import numpy as np
import ml_dtypes


def mxq(x, axis, fmt="e4m3"):
    dtype, down = {"e4m3": (ml_dtypes.float8_e4m3fn, 7), "e5m2": (ml_dtypes.float8_e5m2, 14)}[fmt]
    v = np.moveaxis(np.asarray(x, np.float32).astype(ml_dtypes.bfloat16).astype(np.float64), axis, -1)
    blocks = v.reshape(v.shape[:-1] + (-1, 32))
    amax = np.abs(blocks).max(-1, keepdims=True)
    byte = np.maximum(np.where(amax > 0, np.frexp(amax)[1] - 1 + 127, 0) - down, 1)
    scale = np.exp2(byte - 127.0)
    codes = (blocks / scale).astype(np.float32).astype(dtype).astype(np.float64)
    return np.moveaxis((codes * scale).reshape(v.shape), -1, axis)


WIDE = False


def mx_kscale(k):
    if not WIDE:
        return np.ones(k)
    levels = np.array([10, -10, 5, -5, 0])
    if k % 512:
        return np.exp2(np.random.permutation(np.resize(levels, k // 32))).repeat(32)
    a = np.empty((k // 512, 16))
    for p in range(k // 512):
        a[p, :8] = np.random.permutation(np.resize(levels, 8))
        for g in range(8):
            far = levels[np.abs(levels - a[p, g]) >= 10]
            a[p, g + 8] = far[np.random.randint(len(far))]
    return np.exp2(a.ravel()).repeat(32)


def f64(x):
    return np.asarray(x).astype(np.float64)


def striped(idx):
    return np.tile(np.asarray(idx).reshape(-1, 16).T, (8, 1)).astype(np.uint16)


def unstriped(offs):
    return offs[:16].T.reshape(-1).astype(np.int64)


E2M1 = np.array([0.0, 0.5, 1.0, 1.5, 2.0, 3.0, 4.0, 6.0, -0.0, -0.5, -1.0, -1.5, -2.0, -3.0, -4.0, -6.0])


def pack_weight(w, fmt):
    k, n = w.shape
    w = f64(np.asarray(w, np.float32).astype(ml_dtypes.bfloat16)).reshape(k // 32, 32, n)
    amax = np.abs(w).max(1)
    if fmt == "e4m3":
        byte = np.frexp(amax)[1] - 1 + 127 - 7
    else:
        mant, ex = np.frexp(amax / 6.0)
        byte = np.where(mant > 0.5, ex, ex - 1) + 127
    byte = np.clip(np.where(amax > 0, byte, 1), 1, 254)
    scaled = (w * np.exp2(127.0 - byte)[:, None, :]).reshape(k, n).astype(np.float32)
    by_word = np.ascontiguousarray(scaled.reshape(k // 512, 128, 4, n).transpose(0, 1, 3, 2))
    if fmt == "e4m3":
        words = by_word.astype(ml_dtypes.float8_e4m3fn).view(np.uint8)
    else:
        c = by_word.astype(ml_dtypes.float4_e2m1fn).view(np.uint8) & 0xF
        words = (c[..., 0::2] | (c[..., 1::2] << 4)).reshape(k // 512, 128, 2 * n)
    return np.ascontiguousarray(words), np.ascontiguousarray(byte.astype(np.uint8).reshape(k // 512, 16, n))


def unpack_weight(words, scales, fmt):
    g, _, n = scales.shape
    words = np.ascontiguousarray(words).reshape(g, 128, n, -1)
    if fmt == "e4m3":
        vals = words.view(ml_dtypes.float8_e4m3fn).astype(np.float64)
    else:
        nib = np.empty((g, 128, n, 4), np.uint8)
        nib[..., 0::2] = words & 0xF
        nib[..., 1::2] = words >> 4
        vals = E2M1[nib]
    vals = vals * np.repeat(np.exp2(scales.astype(np.float64) - 127.0), 8, axis=1)[..., None]
    return vals.transpose(0, 1, 3, 2).reshape(g * 512, n)


def bf(x):
    return np.asarray(x, np.float32).astype(ml_dtypes.bfloat16)


def planes(Y):
    r, m = Y.shape
    b = f64(bf(Y)).reshape(r // 32, 32, m)
    amax = np.abs(b).max(1)
    byte = np.clip(np.where(amax > 0, np.frexp(amax)[1] - 1 + 127 - 7, 1), 1, 254)
    codes = (b * np.exp2(127.0 - byte)[:, None, :]).reshape(r, m).astype(np.float32).astype(ml_dtypes.float8_e4m3fn).view(np.uint8)
    words = codes.reshape(r // 512, 128, 4, m).transpose(0, 1, 3, 2)
    return np.ascontiguousarray(words), np.ascontiguousarray(byte.astype(np.uint8).reshape(r // 512, 16, m))


K, T, J, N = 1024, 2048, 512, 512


def setup_inputs():
    n = np.random.standard_normal
    idx = np.random.permutation(T)[:J]
    fk = mx_kscale(K)
    xqp = pack_weight(n((K, T)) / fk[:, None], "e2m1")
    wsp = pack_weight(n((K, N)) * 1 / np.sqrt(K) * fk[:, None], "e4m3")
    return {
        "xq_words": xqp[0],
        "xq_scales": xqp[1],
        "ea": (n((K, N)) * 1 / np.sqrt(K) * fk[:, None]).astype(np.float32),
        "eb": (n((K, N)) * 1 / np.sqrt(K) * fk[:, None]).astype(np.float32),
        "sh": (np.random.uniform(0.2, 0.8, (1, N))).astype(np.float32),
        "ws_words": wsp[0],
        "ws_scales": wsp[1],
        "offs": striped(idx),
    }


def reference(xq_words, xq_scales, ea, eb, sh, ws_words, ws_scales, offs):
    idx = unstriped(offs)
    xqu = unpack_weight(xq_words, xq_scales, "e2m1")
    wsu = unpack_weight(ws_words, ws_scales, "e4m3")
    em = f64(eb) + f64(sh) * (f64(ea) - f64(eb))
    emq = mxq(em, 0, "e4m3")
    xqidxg = xqu[:, idx]
    y = emq.T @ xqidxg + wsu.T @ xqidxg
    words, scales = planes(y)
    return y, words, scales

@@ -1,0 +1,249 @@
+from contextlib import ExitStack
+
+import concourse.mybir as mybir
+from concourse.masks import make_identity
+
+K, T, J, N = 1024, 2048, 512, 512
+FLOPS = 2 * 2 * K * N * J
+
+F32 = mybir.dt.float32
+BF16 = mybir.dt.bfloat16
+I32 = mybir.dt.int32
+U32 = mybir.dt.uint32
+U16 = mybir.dt.uint16
+U8 = mybir.dt.uint8
+FP8X4 = mybir.dt.float8_e4m3fn_x4
+FP4X4 = mybir.dt.float4_e2m1fn_x4
+MULT = mybir.AluOpType.mult
+ADD = mybir.AluOpType.add
+COPY = mybir.ActivationFunctionType.Copy
+
+P = 128
+PASSES = 2
+SPLIT = 384
+
+
+def tile_list_merged_experts_pl_kernel(
+    tc, xq_words, xq_scales, ea, eb, sh, ws_words, ws_scales, offs, out_0, out_1, out_2
+):
+    nc = tc.nc
+    with ExitStack() as ctx:
+        keep = ctx.enter_context(tc.tile_pool(name="keep", bufs=1))
+        acc_pool = ctx.enter_context(tc.psum_pool(name="acc", bufs=1))
+        turn_pool = ctx.enter_context(tc.psum_pool(name="turn", bufs=4))
+
+        def sb(shape, dtype, name):
+            return keep.tile(shape, dtype, name=name, align_bytes=64)
+
+        offsets = keep.tile([P, J // 16], U16, name="offsets")
+        sh_rows = sb([P, P], F32, "sh_rows")
+        xs_table = sb([P, PASSES * T], U8, "xs_table")
+        ws_plane_raw = sb([P, PASSES * N], U8, "ws_plane_raw")
+        x_plane = [sb([P, J], U8, "x_plane%d" % g) for g in range(PASSES)]
+        ident = sb([P, P], F32, "ident")
+
+        nc.vector.memset(sh_rows[:], 0.0)
+        nc.vector.memset(xs_table[:].bitcast(I32), 0)
+        nc.vector.memset(ws_plane_raw[:].bitcast(I32), 0)
+        make_identity(nc, ident[:])
+
+        ea_v = ea.rearrange("(g p u e) n -> g u p (e n)", g=PASSES, u=2, e=2)
+        eb_v = eb.rearrange("(g p u e) n -> g u p (e n)", g=PASSES, u=2, e=2)
+        ea_sb, eb_sb, x_table, ws_raw = {}, {}, {}, {}
+
+        def load_expert(tiles, view, g, u, name):
+            tiles[g, u] = sb([P, 2 * N], F32, "%s%d%d" % (name, g, u))
+            nc.sync.dma_start(tiles[g, u][:], view[g, u])
+
+        def load_experts(g, u):
+            load_expert(eb_sb, eb_v, g, u, "eb")
+            load_expert(ea_sb, ea_v, g, u, "ea")
+
+        def load_tokens(g):
+            x_table[g] = sb([P, T], U16, "x_table%d" % g)
+            nc.sync.dma_start(x_table[g][:].bitcast(I32), xq_words[g].bitcast(I32))
+
+        def load_shared(g):
+            ws_raw[g] = sb([P, N], I32, "ws_raw%d" % g)
+            nc.sync.dma_start(ws_raw[g][:], ws_words[g].rearrange("p n t -> p (n t)").bitcast(I32))
+
+        def load_scale_rows(tile, rows):
+            for quad in range(4):
+                nc.sync.dma_start(
+                    tile[32 * quad : 32 * quad + 4, :].bitcast(I32).rearrange("q (g w) -> q g w", g=PASSES),
+                    rows[:, 4 * quad : 4 * quad + 4, :].bitcast(I32).rearrange("g q w -> q g w"),
+                )
+
+        nc.sync.dma_start(offsets[:], offs)
+        nc.sync.dma_start(sh_rows[0:4, :], sh.rearrange("o (c q) -> (o c) q", c=4))
+        load_experts(0, 0)
+        load_expert(eb_sb, eb_v, 0, 1, "eb")
+        load_scale_rows(xs_table, xq_scales)
+        load_expert(ea_sb, ea_v, 0, 1, "ea")
+        load_tokens(0)
+        load_expert(eb_sb, eb_v, 1, 0, "eb")
+        load_shared(0)
+        load_scale_rows(ws_plane_raw, ws_scales)
+        load_expert(ea_sb, ea_v, 1, 0, "ea")
+        load_tokens(1)
+        load_experts(1, 1)
+        load_shared(1)
+
+        sh_bank = turn_pool.tile([P, 512], F32, tag="turn", name="sh_bank")
+        nc.tensor.transpose(sh_bank[:, 0:P], sh_rows[:], ident[:])
+        share_a = sb([P, 4], F32, "share_a")
+        share_b = sb([P, 4], F32, "share_b")
+        nc.vector.tensor_scalar(share_b[:], sh_bank[:, 0:4], -1.0, 1.0, MULT, ADD)
+        nc.vector.tensor_copy(share_a[:], sh_bank[:, 0:4])
+
+        def gather_token_scales(g):
+            nc.vector.tensor_copy(x_plane[g][:], xs_table[:, g * T : (g + 1) * T].indirect(offsets[:]))
+
+        x_picked = {}
+
+        def gather_tokens(g):
+            x_picked[g] = sb([P, J], U16, "x_picked%d" % g)
+            nc.vector.tensor_copy(x_picked[g][:], x_table[g][:].indirect(offsets[:]))
+
+        ws_plane = sb([P, PASSES * N], U8, "ws_plane")
+        ws_codes = {}
+
+        def deal_shared(g):
+            ws_codes[g] = sb([P, N], I32, "ws_codes%d" % g)
+            nc.vector.tensor_copy(
+                ws_codes[g][:].rearrange("p (t b i) -> p b t i", t=4, i=4),
+                ws_raw[g][:].rearrange("p (b i t) -> p b t i", t=4, i=4),
+            )
+
+        acc = [acc_pool.tile([P, J], F32, name="acc%d" % t) for t in range(4)]
+
+        def multiply(codes, plane, g, start, stop):
+            for t in range(4):
+                cols = slice(t * P, (t + 1) * P)
+                nc.tensor.matmul_mx(
+                    acc[t][:],
+                    lhsT=codes[:, cols].bitcast(FP8X4),
+                    lhsT_scale=plane[:, cols],
+                    rhs=x_picked[g][:].bitcast(FP4X4),
+                    rhs_scale=x_plane[g][:],
+                    start=start,
+                    stop=stop,
+                )
+
+        em_turned, grouped = {}, {}
+
+        def turn_in(src, pair, name):
+            bank = turn_pool.tile([P, 512], F32, tag="turn", name=name)
+            for h in range(2):
+                c = 2 * pair + h
+                for e in range(2):
+                    col = e * N + c * P
+                    at = (2 * h + e) * P
+                    nc.tensor.transpose(bank[:, at : at + P], src[:, col : col + P], ident[:])
+            return bank
+
+        def mix(g, u):
+            part_b = {}
+            for pair in range(2):
+                bank = turn_in(eb_sb[g, u], pair, "b_bank%d%d%d" % (g, u, pair))
+                for h in range(2):
+                    c = 2 * pair + h
+                    part_b[c] = sb([P, 2 * P], F32, "part_b%d%d%d" % (g, u, c))
+                    nc.scalar.activation(
+                        part_b[c][:].rearrange("q (p e) -> q p e", e=2),
+                        bank[:, h * 2 * P : (h + 1) * 2 * P].rearrange("q (e p) -> q p e", e=2),
+                        COPY,
+                        scale=share_b[:, c : c + 1],
+                    )
+            for pair in range(2):
+                bank = turn_in(ea_sb[g, u], pair, "a_bank%d%d%d" % (g, u, pair))
+                for h in range(2):
+                    c = 2 * pair + h
+                    if u == 0:
+                        em_turned[g, c] = sb([P, 4 * P], BF16, "em_turned%d%d" % (g, c))
+                    nc.vector.scalar_tensor_tensor(
+                        em_turned[g, c][:, u * 2 * P : (u + 1) * 2 * P].rearrange("q (p e) -> q p e", e=2),
+                        bank[:, h * 2 * P : (h + 1) * 2 * P].rearrange("q (e p) -> q p e", e=2),
+                        share_a[:, c : c + 1],
+                        part_b[c][:].rearrange("q (p e) -> q p e", e=2),
+                        MULT,
+                        ADD,
+                    )
+
+        def turn_back(g):
+            grouped[g] = sb([P, 4 * N], BF16, "grouped%d" % g)
+            words_out = grouped[g][:].bitcast(F32).rearrange("p (t c m u) -> p c t m u", t=4, c=4, u=2)
+            for c in range(4):
+                bank = turn_pool.tile([P, 512], F32, tag="turn", name="back%d%d" % (g, c))
+                words = em_turned[g, c][:].bitcast(F32)
+                for u in range(2):
+                    nc.tensor.transpose(bank[:, u * P : (u + 1) * P], words[:, u * P : (u + 1) * P], ident[:])
+                nc.scalar.copy(words_out[:, c], bank[:, 0 : 2 * P].rearrange("p (u m t) -> p t m u", u=2, t=4))
+
+        em_codes, em_plane = {}, {}
+
+        def quantise(g):
+            em_codes[g] = sb([P, N], U32, "em_codes%d" % g)
+            em_plane[g] = sb([P, N], U8, "em_plane%d" % g)
+            for t in range(4):
+                cols = slice(t * P, (t + 1) * P)
+                nc.vector.quantize_mx(
+                    em_codes[g][:, cols].bitcast(FP8X4),
+                    em_plane[g][:, cols],
+                    grouped[g][:, t * 4 * P : (t + 1) * 4 * P],
+                )
+
+        mix(0, 0)
+        mix(0, 1)
+        gather_token_scales(0)
+        turn_back(0)
+        gather_tokens(0)
+        quantise(0)
+        gather_token_scales(1)
+        mix(1, 0)
+        multiply(em_codes[0], em_plane[0], 0, True, False)
+        nc.vector.tensor_copy(
+            ws_plane[:].rearrange("p (g t m) -> p g t m", g=PASSES, t=4),
+            ws_plane_raw[:].rearrange("p (g m t) -> p g t m", g=PASSES, t=4),
+        )
+        deal_shared(0)
+        gather_tokens(1)
+        mix(1, 1)
+        multiply(ws_codes[0], ws_plane[:, 0:N], 0, False, False)
+        turn_back(1)
+        deal_shared(1)
+        multiply(ws_codes[1], ws_plane[:, N : 2 * N], 1, False, False)
+        quantise(1)
+        multiply(em_codes[1], em_plane[1], 1, False, True)
+
+        y = sb([P, 4 * J], F32, "y")
+        out_rows = out_0.rearrange("(p t) j -> t p j", t=4)
+        for t in range(4):
+            cols = slice(t * J, (t + 1) * J)
+            if t % 2 == 0:
+                nc.scalar.copy(y[:, cols], acc[t][:])
+            else:
+                nc.vector.tensor_copy(y[:, cols], acc[t][:])
+            nc.sync.dma_start(out_rows[t], y[:, cols])
+
+        y_codes = sb([P, J], U32, "y_codes")
+        y_plane = sb([P, J], U8, "y_plane")
+        y_by_token = y[:].rearrange("p (t b i) -> p b t i", t=4, i=4)
+        for lo, hi, engine in ((0, 256, "v"), (256, SPLIT, "v"), (SPLIT, J, "s")):
+            y_grouped = sb([P, 4 * (hi - lo)], BF16, "y_grouped%d" % lo)
+            dst = y_grouped[:].rearrange("p (b i t) -> p b t i", t=4, i=4)
+            src = y_by_token[:, lo // 4 : hi // 4]
+            if engine == "v":
+                nc.vector.tensor_copy(dst, src)
+            else:
+                nc.scalar.copy(dst, src)
+            nc.vector.quantize_mx(y_codes[:, lo:hi].bitcast(FP8X4), y_plane[:, lo:hi], y_grouped[:])
+        nc.sync.dma_start(
+            out_1[0].rearrange("p j t -> p (j t)").bitcast(I32), y_codes[:].bitcast(I32)
+        )
+        for quad in range(4):
+            queue = nc.scalar if quad % 2 == 0 else nc.sync
+            queue.dma_start(
+                out_2[0, 4 * quad : 4 * quad + 4, :].bitcast(I32),
+                y_plane[32 * quad : 32 * quad + 4, :].bitcast(I32),
+            )

@@ -20,7 +20,7 @@ COPY = mybir.ActivationFunctionType.Copy
 
 P = 128
 PASSES = 2
-SPLIT = 384
+TURNED = (2, 2)
 
 
 def tile_list_merged_experts_pl_kernel(
@@ -30,21 +30,24 @@ def tile_list_merged_experts_pl_kernel(
     with ExitStack() as ctx:
         keep = ctx.enter_context(tc.tile_pool(name="keep", bufs=1))
         acc_pool = ctx.enter_context(tc.psum_pool(name="acc", bufs=1))
-        turn_pool = ctx.enter_context(tc.psum_pool(name="turn", bufs=4))
+        turn_pool = ctx.enter_context(tc.psum_pool(name="turn", bufs=3))
 
         def sb(shape, dtype, name):
             return keep.tile(shape, dtype, name=name, align_bytes=64)
 
         offsets = keep.tile([P, J // 16], U16, name="offsets")
         sh_rows = sb([P, P], F32, "sh_rows")
-        xs_table = sb([P, PASSES * T], U8, "xs_table")
+        xs_table = sb([P, T], U8, "xs_table")
         ws_plane_raw = sb([P, PASSES * N], U8, "ws_plane_raw")
         x_plane = [sb([P, J], U8, "x_plane%d" % g) for g in range(PASSES)]
         ident = sb([P, P], F32, "ident")
 
         nc.vector.memset(sh_rows[:], 0.0)
-        nc.vector.memset(xs_table[:].bitcast(I32), 0)
+        nc.vector.memset(xs_table[32:64, :].bitcast(I32), 0)
+        nc.vector.memset(xs_table[64:128, :].bitcast(I32), 0)
         nc.vector.memset(ws_plane_raw[:].bitcast(I32), 0)
+        for g in range(PASSES):
+            nc.vector.memset(x_plane[g][:].bitcast(I32), 0)
         make_identity(nc, ident[:])
 
         ea_v = ea.rearrange("(g p u e) n -> g u p (e n)", g=PASSES, u=2, e=2)
@@ -67,26 +70,46 @@ def tile_list_merged_experts_pl_kernel(
             ws_raw[g] = sb([P, N], I32, "ws_raw%d" % g)
             nc.sync.dma_start(ws_raw[g][:], ws_words[g].rearrange("p n t -> p (n t)").bitcast(I32))
 
-        def load_scale_rows(tile, rows):
-            for quad in range(4):
-                nc.sync.dma_start(
-                    tile[32 * quad : 32 * quad + 4, :].bitcast(I32).rearrange("q (g w) -> q g w", g=PASSES),
-                    rows[:, 4 * quad : 4 * quad + 4, :].bitcast(I32).rearrange("g q w -> q g w"),
-                )
+        def load_shared_scales(quad):
+            nc.sync.dma_start(
+                ws_plane_raw[32 * quad : 32 * quad + 4, :].bitcast(I32).rearrange("q (g w) -> q g w", g=PASSES),
+                ws_scales[:, 4 * quad : 4 * quad + 4, :].bitcast(I32).rearrange("g q w -> q g w"),
+            )
+
+        xs_picked = sb([P, J], U8, "xs_picked")
+
+        def place_token_scales(queue, g, quad):
+            row = 16 * g + 4 * quad
+            queue.dma_start(
+                x_plane[g][32 * quad : 32 * quad + 4, :].bitcast(I32),
+                xs_picked[row : row + 4, :].bitcast(I32),
+            )
 
         nc.sync.dma_start(offsets[:], offs)
+        nc.sync.dma_start(
+            xs_table[0:32, :].bitcast(I32), xq_scales.rearrange("g q t -> (g q) t").bitcast(I32)
+        )
         nc.sync.dma_start(sh_rows[0:4, :], sh.rearrange("o (c q) -> (o c) q", c=4))
         load_experts(0, 0)
-        load_expert(eb_sb, eb_v, 0, 1, "eb")
-        load_scale_rows(xs_table, xq_scales)
-        load_expert(ea_sb, ea_v, 0, 1, "ea")
+        load_experts(0, 1)
         load_tokens(0)
+        nc.vector.tensor_copy(xs_picked[:], xs_table[:].indirect(offsets[:]))
+        for quad in range(4):
+            place_token_scales(nc.gpsimd, 0, quad)
+        load_shared_scales(0)
         load_expert(eb_sb, eb_v, 1, 0, "eb")
+        load_shared_scales(1)
         load_shared(0)
-        load_scale_rows(ws_plane_raw, ws_scales)
+        load_shared_scales(2)
         load_expert(ea_sb, ea_v, 1, 0, "ea")
+        load_shared_scales(3)
+        place_token_scales(nc.sync, 1, 0)
         load_tokens(1)
-        load_experts(1, 1)
+        place_token_scales(nc.sync, 1, 1)
+        load_expert(eb_sb, eb_v, 1, 1, "eb")
+        place_token_scales(nc.sync, 1, 2)
+        place_token_scales(nc.sync, 1, 3)
+        load_expert(ea_sb, ea_v, 1, 1, "ea")
         load_shared(1)
 
         sh_bank = turn_pool.tile([P, 512], F32, tag="turn", name="sh_bank")
@@ -96,8 +119,15 @@ def tile_list_merged_experts_pl_kernel(
         nc.vector.tensor_scalar(share_b[:], sh_bank[:, 0:4], -1.0, 1.0, MULT, ADD)
         nc.vector.tensor_copy(share_a[:], sh_bank[:, 0:4])
 
-        def gather_token_scales(g):
-            nc.vector.tensor_copy(x_plane[g][:], xs_table[:, g * T : (g + 1) * T].indirect(offsets[:]))
+        first_plain = min(TURNED)
+        plain_max = N - first_plain * P
+        share_rows = acc_pool.tile([P, 2 * plain_max], F32, name="share_rows")
+        for half, share in enumerate((share_b, share_a)):
+            for c in range(first_plain, 4):
+                at = half * plain_max + (c - first_plain) * P
+                nc.tensor.transpose(
+                    share_rows[:, at : at + P], share[:, c : c + 1].to_broadcast([P, P]), ident[:]
+                )
 
         x_picked = {}
 
@@ -132,22 +162,36 @@ def tile_list_merged_experts_pl_kernel(
 
         em_turned, grouped = {}, {}
 
-        def turn_in(src, pair, name):
+        def turn_in(src, chunks, name):
             bank = turn_pool.tile([P, 512], F32, tag="turn", name=name)
-            for h in range(2):
-                c = 2 * pair + h
+            for h, c in enumerate(chunks):
                 for e in range(2):
                     col = e * N + c * P
                     at = (2 * h + e) * P
                     nc.tensor.transpose(bank[:, at : at + P], src[:, col : col + P], ident[:])
             return bank
 
+        em_plain = {}
+
+        def scale_plain(src, half, g, name):
+            width = N - TURNED[g] * P
+            end = (half + 1) * plain_max
+            part = sb([P, 2 * width], F32, name)
+            nc.vector.tensor_tensor(
+                part[:].rearrange("p (e n) -> p e n", e=2),
+                src[:].rearrange("p (e n) -> p e n", e=2)[:, :, N - width : N],
+                share_rows[:, end - width : end].unsqueeze(1).to_broadcast([P, 2, width]),
+                MULT,
+            )
+            return part
+
         def mix(g, u):
             part_b = {}
-            for pair in range(2):
-                bank = turn_in(eb_sb[g, u], pair, "b_bank%d%d%d" % (g, u, pair))
-                for h in range(2):
-                    c = 2 * pair + h
+            groups = [range(c, min(c + 2, TURNED[g])) for c in range(0, TURNED[g], 2)]
+            width = N - TURNED[g] * P
+            for chunks in groups:
+                bank = turn_in(eb_sb[g, u], chunks, "b_bank%d%d%d" % (g, u, chunks[0]))
+                for h, c in enumerate(chunks):
                     part_b[c] = sb([P, 2 * P], F32, "part_b%d%d%d" % (g, u, c))
                     nc.scalar.activation(
                         part_b[c][:].rearrange("q (p e) -> q p e", e=2),
@@ -155,10 +199,11 @@ def tile_list_merged_experts_pl_kernel(
                         COPY,
                         scale=share_b[:, c : c + 1],
                     )
-            for pair in range(2):
-                bank = turn_in(ea_sb[g, u], pair, "a_bank%d%d%d" % (g, u, pair))
-                for h in range(2):
-                    c = 2 * pair + h
+            plain_b = scale_plain(eb_sb[g, u], 0, g, "plain_b%d%d" % (g, u))
+            plain_a = scale_plain(ea_sb[g, u], 1, g, "plain_a%d%d" % (g, u))
+            for chunks in groups:
+                bank = turn_in(ea_sb[g, u], chunks, "a_bank%d%d%d" % (g, u, chunks[0]))
+                for h, c in enumerate(chunks):
                     if u == 0:
                         em_turned[g, c] = sb([P, 4 * P], BF16, "em_turned%d%d" % (g, c))
                     nc.vector.scalar_tensor_tensor(
@@ -169,37 +214,46 @@ def tile_list_merged_experts_pl_kernel(
                         MULT,
                         ADD,
                     )
+            if u == 0:
+                em_plain[g] = sb([P, 4 * width], F32, "em_plain%d" % g)
+            nc.vector.tensor_tensor(
+                em_plain[g][:, u * 2 * width : (u + 1) * 2 * width], plain_a[:], plain_b[:], ADD
+            )
 
         def turn_back(g):
             grouped[g] = sb([P, 4 * N], BF16, "grouped%d" % g)
             words_out = grouped[g][:].bitcast(F32).rearrange("p (t c m u) -> p c t m u", t=4, c=4, u=2)
-            for c in range(4):
+            for c in range(TURNED[g]):
                 bank = turn_pool.tile([P, 512], F32, tag="turn", name="back%d%d" % (g, c))
                 words = em_turned[g, c][:].bitcast(F32)
                 for u in range(2):
                     nc.tensor.transpose(bank[:, u * P : (u + 1) * P], words[:, u * P : (u + 1) * P], ident[:])
                 nc.scalar.copy(words_out[:, c], bank[:, 0 : 2 * P].rearrange("p (u m t) -> p t m u", u=2, t=4))
+            values_out = grouped[g][:].rearrange("p (t c m r) -> p c m t r", t=4, c=4, r=4)
+            values_in = em_plain[g][:].rearrange("p (r c m t) -> p c m t r", r=4, m=32, t=4)
+            for c in range(TURNED[g], 4):
+                engine = nc.vector.tensor_copy if g == 1 and c == 3 else nc.scalar.copy
+                engine(values_out[:, c], values_in[:, c - TURNED[g]])
 
         em_codes, em_plane = {}, {}
 
         def quantise(g):
             em_codes[g] = sb([P, N], U32, "em_codes%d" % g)
             em_plane[g] = sb([P, N], U8, "em_plane%d" % g)
-            for t in range(4):
-                cols = slice(t * P, (t + 1) * P)
+            width = N if g == 0 else P
+            for lo in range(0, N, width):
+                cols = slice(lo, lo + width)
                 nc.vector.quantize_mx(
                     em_codes[g][:, cols].bitcast(FP8X4),
                     em_plane[g][:, cols],
-                    grouped[g][:, t * 4 * P : (t + 1) * 4 * P],
+                    grouped[g][:, 4 * lo : 4 * (lo + width)],
                 )
 
         mix(0, 0)
         mix(0, 1)
-        gather_token_scales(0)
         turn_back(0)
         gather_tokens(0)
         quantise(0)
-        gather_token_scales(1)
         mix(1, 0)
         multiply(em_codes[0], em_plane[0], 0, True, False)
         nc.vector.tensor_copy(
@@ -218,29 +272,31 @@ def tile_list_merged_experts_pl_kernel(
 
         y = sb([P, 4 * J], F32, "y")
         out_rows = out_0.rearrange("(p t) j -> t p j", t=4)
+        half = J // 2
         for t in range(4):
             cols = slice(t * J, (t + 1) * J)
             if t % 2 == 0:
                 nc.scalar.copy(y[:, cols], acc[t][:])
-            else:
+            elif t == 1:
                 nc.vector.tensor_copy(y[:, cols], acc[t][:])
+            else:
+                for lo in (0, half):
+                    nc.vector.tensor_copy(y[:, t * J + lo : t * J + lo + half], acc[t][:, lo : lo + half])
             nc.sync.dma_start(out_rows[t], y[:, cols])
 
         y_codes = sb([P, J], U32, "y_codes")
         y_plane = sb([P, J], U8, "y_plane")
         y_by_token = y[:].rearrange("p (t b i) -> p b t i", t=4, i=4)
-        for lo, hi, engine in ((0, 256, "v"), (256, SPLIT, "v"), (SPLIT, J, "s")):
-            y_grouped = sb([P, 4 * (hi - lo)], BF16, "y_grouped%d" % lo)
-            dst = y_grouped[:].rearrange("p (b i t) -> p b t i", t=4, i=4)
-            src = y_by_token[:, lo // 4 : hi // 4]
-            if engine == "v":
-                nc.vector.tensor_copy(dst, src)
-            else:
-                nc.scalar.copy(dst, src)
-            nc.vector.quantize_mx(y_codes[:, lo:hi].bitcast(FP8X4), y_plane[:, lo:hi], y_grouped[:])
-        nc.sync.dma_start(
-            out_1[0].rearrange("p j t -> p (j t)").bitcast(I32), y_codes[:].bitcast(I32)
-        )
+        y_grouped = {}
+        for lo, hi, copy in ((0, P, nc.scalar.copy), (half, J, nc.vector.tensor_copy), (P, half, nc.scalar.copy)):
+            y_grouped[lo] = sb([P, 4 * (hi - lo)], BF16, "y_grouped%d" % lo)
+            copy(y_grouped[lo][:].rearrange("p (b i t) -> p b t i", t=4, i=4), y_by_token[:, lo // 4 : hi // 4])
+        out_words = out_1[0].rearrange("p j t -> p (j t)").bitcast(I32)
+        for lo, hi in ((0, P), (half, J), (P, half)):
+            nc.vector.quantize_mx(y_codes[:, lo:hi].bitcast(FP8X4), y_plane[:, lo:hi], y_grouped[lo][:])
+            if lo > 0:
+                stored = slice(half, J) if lo == half else slice(0, half)
+                nc.sync.dma_start(out_words[:, stored], y_codes[:, stored].bitcast(I32))
         for quad in range(4):
             queue = nc.scalar if quad % 2 == 0 else nc.sync
             queue.dma_start(

from contextlib import ExitStack

import concourse.mybir as mybir
from concourse.masks import make_identity

K, T, J, N = 1024, 2048, 512, 512
FLOPS = 2 * 2 * K * N * J

F32 = mybir.dt.float32
BF16 = mybir.dt.bfloat16
I32 = mybir.dt.int32
U32 = mybir.dt.uint32
U16 = mybir.dt.uint16
U8 = mybir.dt.uint8
FP8X4 = mybir.dt.float8_e4m3fn_x4
FP4X4 = mybir.dt.float4_e2m1fn_x4
MULT = mybir.AluOpType.mult
ADD = mybir.AluOpType.add
COPY = mybir.ActivationFunctionType.Copy

P = 128
PASSES = 2
TURNED = (2, 2)


def tile_list_merged_experts_pl_kernel(
    tc, xq_words, xq_scales, ea, eb, sh, ws_words, ws_scales, offs, out_0, out_1, out_2
):
    nc = tc.nc
    with ExitStack() as ctx:
        keep = ctx.enter_context(tc.tile_pool(name="keep", bufs=1))
        acc_pool = ctx.enter_context(tc.psum_pool(name="acc", bufs=1))
        turn_pool = ctx.enter_context(tc.psum_pool(name="turn", bufs=3))

        def sb(shape, dtype, name):
            return keep.tile(shape, dtype, name=name, align_bytes=64)

        offsets = keep.tile([P, J // 16], U16, name="offsets")
        sh_rows = sb([P, P], F32, "sh_rows")
        xs_table = sb([P, T], U8, "xs_table")
        ws_plane_raw = sb([P, PASSES * N], U8, "ws_plane_raw")
        x_plane = [sb([P, J], U8, "x_plane%d" % g) for g in range(PASSES)]
        ident = sb([P, P], F32, "ident")

        nc.vector.memset(sh_rows[:], 0.0)
        nc.vector.memset(xs_table[32:64, :].bitcast(I32), 0)
        nc.vector.memset(xs_table[64:128, :].bitcast(I32), 0)
        nc.vector.memset(ws_plane_raw[:].bitcast(I32), 0)
        for g in range(PASSES):
            nc.vector.memset(x_plane[g][:].bitcast(I32), 0)
        make_identity(nc, ident[:])

        ea_v = ea.rearrange("(g p u e) n -> g u p (e n)", g=PASSES, u=2, e=2)
        eb_v = eb.rearrange("(g p u e) n -> g u p (e n)", g=PASSES, u=2, e=2)
        ea_sb, eb_sb, x_table, ws_raw = {}, {}, {}, {}

        def load_expert(tiles, view, g, u, name):
            tiles[g, u] = sb([P, 2 * N], F32, "%s%d%d" % (name, g, u))
            nc.sync.dma_start(tiles[g, u][:], view[g, u])

        def load_experts(g, u):
            load_expert(eb_sb, eb_v, g, u, "eb")
            load_expert(ea_sb, ea_v, g, u, "ea")

        def load_tokens(g):
            x_table[g] = sb([P, T], U16, "x_table%d" % g)
            nc.sync.dma_start(x_table[g][:].bitcast(I32), xq_words[g].bitcast(I32))

        def load_shared(g):
            ws_raw[g] = sb([P, N], I32, "ws_raw%d" % g)
            nc.sync.dma_start(ws_raw[g][:], ws_words[g].rearrange("p n t -> p (n t)").bitcast(I32))

        def load_shared_scales(quad):
            nc.sync.dma_start(
                ws_plane_raw[32 * quad : 32 * quad + 4, :].bitcast(I32).rearrange("q (g w) -> q g w", g=PASSES),
                ws_scales[:, 4 * quad : 4 * quad + 4, :].bitcast(I32).rearrange("g q w -> q g w"),
            )

        xs_picked = sb([P, J], U8, "xs_picked")

        def place_token_scales(queue, g, quad):
            row = 16 * g + 4 * quad
            queue.dma_start(
                x_plane[g][32 * quad : 32 * quad + 4, :].bitcast(I32),
                xs_picked[row : row + 4, :].bitcast(I32),
            )

        nc.sync.dma_start(offsets[:], offs)
        nc.sync.dma_start(
            xs_table[0:32, :].bitcast(I32), xq_scales.rearrange("g q t -> (g q) t").bitcast(I32)
        )
        nc.sync.dma_start(sh_rows[0:4, :], sh.rearrange("o (c q) -> (o c) q", c=4))
        load_experts(0, 0)
        load_experts(0, 1)
        load_tokens(0)
        nc.vector.tensor_copy(xs_picked[:], xs_table[:].indirect(offsets[:]))
        for quad in range(4):
            place_token_scales(nc.gpsimd, 0, quad)
        load_shared_scales(0)
        load_expert(eb_sb, eb_v, 1, 0, "eb")
        load_shared_scales(1)
        load_shared(0)
        load_shared_scales(2)
        load_expert(ea_sb, ea_v, 1, 0, "ea")
        load_shared_scales(3)
        place_token_scales(nc.sync, 1, 0)
        load_tokens(1)
        place_token_scales(nc.sync, 1, 1)
        load_expert(eb_sb, eb_v, 1, 1, "eb")
        place_token_scales(nc.sync, 1, 2)
        place_token_scales(nc.sync, 1, 3)
        load_expert(ea_sb, ea_v, 1, 1, "ea")
        load_shared(1)

        sh_bank = turn_pool.tile([P, 512], F32, tag="turn", name="sh_bank")
        nc.tensor.transpose(sh_bank[:, 0:P], sh_rows[:], ident[:])
        share_a = sb([P, 4], F32, "share_a")
        share_b = sb([P, 4], F32, "share_b")
        nc.vector.tensor_scalar(share_b[:], sh_bank[:, 0:4], -1.0, 1.0, MULT, ADD)
        nc.vector.tensor_copy(share_a[:], sh_bank[:, 0:4])

        first_plain = min(TURNED)
        plain_max = N - first_plain * P
        share_rows = acc_pool.tile([P, 2 * plain_max], F32, name="share_rows")
        for half, share in enumerate((share_b, share_a)):
            for c in range(first_plain, 4):
                at = half * plain_max + (c - first_plain) * P
                nc.tensor.transpose(
                    share_rows[:, at : at + P], share[:, c : c + 1].to_broadcast([P, P]), ident[:]
                )

        x_picked = {}

        def gather_tokens(g):
            x_picked[g] = sb([P, J], U16, "x_picked%d" % g)
            nc.vector.tensor_copy(x_picked[g][:], x_table[g][:].indirect(offsets[:]))

        ws_plane = sb([P, PASSES * N], U8, "ws_plane")
        ws_codes = {}

        def deal_shared(g):
            ws_codes[g] = sb([P, N], I32, "ws_codes%d" % g)
            nc.vector.tensor_copy(
                ws_codes[g][:].rearrange("p (t b i) -> p b t i", t=4, i=4),
                ws_raw[g][:].rearrange("p (b i t) -> p b t i", t=4, i=4),
            )

        acc = [acc_pool.tile([P, J], F32, name="acc%d" % t) for t in range(4)]

        def multiply(codes, plane, g, start, stop):
            for t in range(4):
                cols = slice(t * P, (t + 1) * P)
                nc.tensor.matmul_mx(
                    acc[t][:],
                    lhsT=codes[:, cols].bitcast(FP8X4),
                    lhsT_scale=plane[:, cols],
                    rhs=x_picked[g][:].bitcast(FP4X4),
                    rhs_scale=x_plane[g][:],
                    start=start,
                    stop=stop,
                )

        em_turned, grouped = {}, {}

        def turn_in(src, chunks, name):
            bank = turn_pool.tile([P, 512], F32, tag="turn", name=name)
            for h, c in enumerate(chunks):
                for e in range(2):
                    col = e * N + c * P
                    at = (2 * h + e) * P
                    nc.tensor.transpose(bank[:, at : at + P], src[:, col : col + P], ident[:])
            return bank

        em_plain = {}

        def scale_plain(src, half, g, name):
            width = N - TURNED[g] * P
            end = (half + 1) * plain_max
            part = sb([P, 2 * width], F32, name)
            nc.vector.tensor_tensor(
                part[:].rearrange("p (e n) -> p e n", e=2),
                src[:].rearrange("p (e n) -> p e n", e=2)[:, :, N - width : N],
                share_rows[:, end - width : end].unsqueeze(1).to_broadcast([P, 2, width]),
                MULT,
            )
            return part

        def mix(g, u):
            part_b = {}
            groups = [range(c, min(c + 2, TURNED[g])) for c in range(0, TURNED[g], 2)]
            width = N - TURNED[g] * P
            for chunks in groups:
                bank = turn_in(eb_sb[g, u], chunks, "b_bank%d%d%d" % (g, u, chunks[0]))
                for h, c in enumerate(chunks):
                    part_b[c] = sb([P, 2 * P], F32, "part_b%d%d%d" % (g, u, c))
                    nc.scalar.activation(
                        part_b[c][:].rearrange("q (p e) -> q p e", e=2),
                        bank[:, h * 2 * P : (h + 1) * 2 * P].rearrange("q (e p) -> q p e", e=2),
                        COPY,
                        scale=share_b[:, c : c + 1],
                    )
            plain_b = scale_plain(eb_sb[g, u], 0, g, "plain_b%d%d" % (g, u))
            plain_a = scale_plain(ea_sb[g, u], 1, g, "plain_a%d%d" % (g, u))
            for chunks in groups:
                bank = turn_in(ea_sb[g, u], chunks, "a_bank%d%d%d" % (g, u, chunks[0]))
                for h, c in enumerate(chunks):
                    if u == 0:
                        em_turned[g, c] = sb([P, 4 * P], BF16, "em_turned%d%d" % (g, c))
                    nc.vector.scalar_tensor_tensor(
                        em_turned[g, c][:, u * 2 * P : (u + 1) * 2 * P].rearrange("q (p e) -> q p e", e=2),
                        bank[:, h * 2 * P : (h + 1) * 2 * P].rearrange("q (e p) -> q p e", e=2),
                        share_a[:, c : c + 1],
                        part_b[c][:].rearrange("q (p e) -> q p e", e=2),
                        MULT,
                        ADD,
                    )
            if u == 0:
                em_plain[g] = sb([P, 4 * width], F32, "em_plain%d" % g)
            nc.vector.tensor_tensor(
                em_plain[g][:, u * 2 * width : (u + 1) * 2 * width], plain_a[:], plain_b[:], ADD
            )

        def turn_back(g):
            grouped[g] = sb([P, 4 * N], BF16, "grouped%d" % g)
            words_out = grouped[g][:].bitcast(F32).rearrange("p (t c m u) -> p c t m u", t=4, c=4, u=2)
            for c in range(TURNED[g]):
                bank = turn_pool.tile([P, 512], F32, tag="turn", name="back%d%d" % (g, c))
                words = em_turned[g, c][:].bitcast(F32)
                for u in range(2):
                    nc.tensor.transpose(bank[:, u * P : (u + 1) * P], words[:, u * P : (u + 1) * P], ident[:])
                nc.scalar.copy(words_out[:, c], bank[:, 0 : 2 * P].rearrange("p (u m t) -> p t m u", u=2, t=4))
            values_out = grouped[g][:].rearrange("p (t c m r) -> p c m t r", t=4, c=4, r=4)
            values_in = em_plain[g][:].rearrange("p (r c m t) -> p c m t r", r=4, m=32, t=4)
            for c in range(TURNED[g], 4):
                engine = nc.vector.tensor_copy if g == 1 and c == 3 else nc.scalar.copy
                engine(values_out[:, c], values_in[:, c - TURNED[g]])

        em_codes, em_plane = {}, {}

        def quantise(g):
            em_codes[g] = sb([P, N], U32, "em_codes%d" % g)
            em_plane[g] = sb([P, N], U8, "em_plane%d" % g)
            width = N if g == 0 else P
            for lo in range(0, N, width):
                cols = slice(lo, lo + width)
                nc.vector.quantize_mx(
                    em_codes[g][:, cols].bitcast(FP8X4),
                    em_plane[g][:, cols],
                    grouped[g][:, 4 * lo : 4 * (lo + width)],
                )

        mix(0, 0)
        mix(0, 1)
        turn_back(0)
        gather_tokens(0)
        quantise(0)
        mix(1, 0)
        multiply(em_codes[0], em_plane[0], 0, True, False)
        nc.vector.tensor_copy(
            ws_plane[:].rearrange("p (g t m) -> p g t m", g=PASSES, t=4),
            ws_plane_raw[:].rearrange("p (g m t) -> p g t m", g=PASSES, t=4),
        )
        deal_shared(0)
        gather_tokens(1)
        mix(1, 1)
        multiply(ws_codes[0], ws_plane[:, 0:N], 0, False, False)
        turn_back(1)
        deal_shared(1)
        multiply(ws_codes[1], ws_plane[:, N : 2 * N], 1, False, False)
        quantise(1)
        multiply(em_codes[1], em_plane[1], 1, False, True)

        y = sb([P, 4 * J], F32, "y")
        out_rows = out_0.rearrange("(p t) j -> t p j", t=4)
        half = J // 2
        for t in range(4):
            cols = slice(t * J, (t + 1) * J)
            if t % 2 == 0:
                nc.scalar.copy(y[:, cols], acc[t][:])
            elif t == 1:
                nc.vector.tensor_copy(y[:, cols], acc[t][:])
            else:
                for lo in (0, half):
                    nc.vector.tensor_copy(y[:, t * J + lo : t * J + lo + half], acc[t][:, lo : lo + half])
            nc.sync.dma_start(out_rows[t], y[:, cols])

        y_codes = sb([P, J], U32, "y_codes")
        y_plane = sb([P, J], U8, "y_plane")
        y_by_token = y[:].rearrange("p (t b i) -> p b t i", t=4, i=4)
        y_grouped = {}
        for lo, hi, copy in ((0, P, nc.scalar.copy), (half, J, nc.vector.tensor_copy), (P, half, nc.scalar.copy)):
            y_grouped[lo] = sb([P, 4 * (hi - lo)], BF16, "y_grouped%d" % lo)
            copy(y_grouped[lo][:].rearrange("p (b i t) -> p b t i", t=4, i=4), y_by_token[:, lo // 4 : hi // 4])
        out_words = out_1[0].rearrange("p j t -> p (j t)").bitcast(I32)
        for lo, hi in ((0, P), (half, J), (P, half)):
            nc.vector.quantize_mx(y_codes[:, lo:hi].bitcast(FP8X4), y_plane[:, lo:hi], y_grouped[lo][:])
            if lo > 0:
                stored = slice(half, J) if lo == half else slice(0, half)
                nc.sync.dma_start(out_words[:, stored], y_codes[:, stored].bitcast(I32))
        for quad in range(4):
            queue = nc.scalar if quad % 2 == 0 else nc.sync
            queue.dma_start(
                out_2[0, 4 * quad : 4 * quad + 4, :].bitcast(I32),
                y_plane[32 * quad : 32 * quad + 4, :].bitcast(I32),
            )
